import numpy as np, ml_dtypes
CORES = [2,3,0,1]
N = 4
ROOT = 1
def setup_inputs(rng):
    return {"x": rng.standard_normal((N, 128, N * 4), dtype=np.float32).astype(ml_dtypes.bfloat16)}
def reference(x):
    return {"y": np.stack([x[ROOT][:, r * 4:(r + 1) * 4] for r in range(N)])}

from concourse.bass import DstId, RemoteDMATransfer

BLOCK = 4
ENGINES = 4

SCRATCH = {
    "stage": ("sbuf", [128, 16], "bfloat16"),
    "land": ("sbuf", [128, 4], "bfloat16"),
}
SEMAPHORES = ["loaded", "read", "arrived", "stored"]


def rank_program(g, core, T, topo):
    rank = T.rank_of(core)
    if rank is None:
        return

    root = T.root
    if rank != root:
        g.wait_ge(T.sem.arrived, ENGINES)
        g.dma_start(T.y[:], T.land[:]).then_inc(T.sem.stored, 16)
        g.wait_ge(T.sem.stored, 16)
        return

    g.dma_start(T.stage[:], T.x[:]).then_inc(T.sem.loaded, 16)
    g.dma_start(T.y[:], T.x[:, root * BLOCK:(root + 1) * BLOCK]).then_inc(T.sem.stored, 16)
    g.wait_ge(T.sem.loaded, 16)

    transfers = []
    for r, dst in enumerate(T.cores):
        if r == root:
            continue
        rid, pid, sengine = topo.addr(dst)
        k = len(transfers)
        transfers.append(RemoteDMATransfer(
            dst_ids=[DstId(rid=rid, pnc=pid)],
            dma_engine_mask=((1 << ENGINES) - 1) << (ENGINES * k),
            remote_sem=T.sem.arrived,
            src=T.stage[:, r * BLOCK:(r + 1) * BLOCK],
            dst=T.land[:],
        ))
    g.remote_dma_fused(transfers, local_sem=T.sem.read)
    g.wait_ge(T.sem.read, ENGINES * len(transfers))
    g.wait_ge(T.sem.stored, 16)
